import numpy as np
import ml_dtypes


def mxq(x, axis, fmt="e4m3"):
    dtype, down = {"e4m3": (ml_dtypes.float8_e4m3fn, 7), "e5m2": (ml_dtypes.float8_e5m2, 14)}[fmt]
    v = np.moveaxis(np.asarray(x, np.float32).astype(ml_dtypes.bfloat16).astype(np.float64), axis, -1)
    blocks = v.reshape(v.shape[:-1] + (-1, 32))
    amax = np.abs(blocks).max(-1, keepdims=True)
    byte = np.maximum(np.where(amax > 0, np.frexp(amax)[1] - 1 + 127, 0) - down, 1)
    scale = np.exp2(byte - 127.0)
    codes = (blocks / scale).astype(np.float32).astype(dtype).astype(np.float64)
    return np.moveaxis((codes * scale).reshape(v.shape), -1, axis)


WIDE = False


def mx_kscale(k):
    if not WIDE:
        return np.ones(k)
    levels = np.array([30, -30])
    if k % 512:
        return np.exp2(np.random.permutation(np.resize(levels, k // 32))).repeat(32)
    a = np.empty((k // 512, 16))
    for p in range(k // 512):
        a[p, :8] = np.random.permutation(np.resize(levels, 8))
        for g in range(8):
            far = levels[np.abs(levels - a[p, g]) >= 10]
            a[p, g + 8] = far[np.random.randint(len(far))]
    return np.exp2(a.ravel()).repeat(32)


def f64(x):
    return np.asarray(x).astype(np.float64)


E2M1 = np.array([0.0, 0.5, 1.0, 1.5, 2.0, 3.0, 4.0, 6.0, -0.0, -0.5, -1.0, -1.5, -2.0, -3.0, -4.0, -6.0])


def pack_weight(w, fmt):
    k, n = w.shape
    w = f64(np.asarray(w, np.float32).astype(ml_dtypes.bfloat16)).reshape(k // 32, 32, n)
    amax = np.abs(w).max(1)
    if fmt == "e4m3":
        byte = np.frexp(amax)[1] - 1 + 127 - 7
    else:
        mant, ex = np.frexp(amax / 6.0)
        byte = np.where(mant > 0.5, ex, ex - 1) + 127
    byte = np.clip(np.where(amax > 0, byte, 1), 1, 254)
    scaled = (w * np.exp2(127.0 - byte)[:, None, :]).reshape(k, n).astype(np.float32)
    by_word = np.ascontiguousarray(scaled.reshape(k // 512, 128, 4, n).transpose(0, 1, 3, 2))
    if fmt == "e4m3":
        words = by_word.astype(ml_dtypes.float8_e4m3fn).view(np.uint8)
    else:
        c = by_word.astype(ml_dtypes.float4_e2m1fn).view(np.uint8) & 0xF
        words = (c[..., 0::2] | (c[..., 1::2] << 4)).reshape(k // 512, 128, 2 * n)
    return np.ascontiguousarray(words), np.ascontiguousarray(byte.astype(np.uint8).reshape(k // 512, 16, n))


def unpack_weight(words, scales, fmt):
    g, _, n = scales.shape
    words = np.ascontiguousarray(words).reshape(g, 128, n, -1)
    if fmt == "e4m3":
        vals = words.view(ml_dtypes.float8_e4m3fn).astype(np.float64)
    else:
        nib = np.empty((g, 128, n, 4), np.uint8)
        nib[..., 0::2] = words & 0xF
        nib[..., 1::2] = words >> 4
        vals = E2M1[nib]
    vals = vals * np.repeat(np.exp2(scales.astype(np.float64) - 127.0), 8, axis=1)[..., None]
    return vals.transpose(0, 1, 3, 2).reshape(g * 512, n)


def bf(x):
    return np.asarray(x, np.float32).astype(ml_dtypes.bfloat16)


def planes(Y):
    r, m = Y.shape
    b = f64(bf(Y)).reshape(r // 32, 32, m)
    amax = np.abs(b).max(1)
    byte = np.clip(np.where(amax > 0, np.frexp(amax)[1] - 1 + 127 - 7, 1), 1, 254)
    codes = (b * np.exp2(127.0 - byte)[:, None, :]).reshape(r, m).astype(np.float32).astype(ml_dtypes.float8_e4m3fn).view(np.uint8)
    words = codes.reshape(r // 512, 128, 4, m).transpose(0, 1, 3, 2)
    return np.ascontiguousarray(words), np.ascontiguousarray(byte.astype(np.uint8).reshape(r // 512, 16, m))


K, T, J, M, N = 512, 512, 512, 512, 512


def setup_inputs():
    n = np.random.standard_normal
    fk = mx_kscale(K)
    fj = mx_kscale(J)
    fm = mx_kscale(M)
    tq = np.exp(2 * n((T, J)))
    xtp = pack_weight(n((K, T)) * 0.4 / fk[:, None], "e2m1")
    wcp = pack_weight(n((K, J)) * 1 / np.sqrt(K) * fk[:, None], "e4m3")
    wop = pack_weight(n((J, N)) * 1 / np.sqrt(J) / fj[:, None], "e2m1")
    wrp = pack_weight(n((K, M)) * 1 / np.sqrt(K) * fk[:, None], "e4m3")
    wbp = pack_weight(n((M, N)) * 1 / np.sqrt(M) / fm[:, None], "e2m1")
    return {
        "xt_words": xtp[0],
        "xt_scales": xtp[1],
        "wc_words": wcp[0],
        "wc_scales": wcp[1],
        "tg": (tq / tq.sum(axis=1, keepdims=True)).astype(np.float32),
        "fj": (np.random.uniform(64.0, 128.0, (J, 1)) * fj[:, None]).astype(np.float32),
        "wo_words": wop[0],
        "wo_scales": wop[1],
        "wr_words": wrp[0],
        "wr_scales": wrp[1],
        "tr1": (1.0 * n((M, T))).astype(np.float32),
        "fm": (np.random.uniform(0.5, 2.0, (M, 1)) * fm[:, None]).astype(np.float32),
        "wb_words": wbp[0],
        "wb_scales": wbp[1],
    }


def reference(xt_words, xt_scales, wc_words, wc_scales, tg, fj, wo_words, wo_scales, wr_words, wr_scales, tr1, fm, wb_words, wb_scales):
    xtu = unpack_weight(xt_words, xt_scales, "e2m1")
    wcu = unpack_weight(wc_words, wc_scales, "e4m3")
    wou = unpack_weight(wo_words, wo_scales, "e2m1")
    wru = unpack_weight(wr_words, wr_scales, "e4m3")
    wbu = unpack_weight(wb_words, wb_scales, "e2m1")
    a = xtu.T @ wcu
    e = np.exp(a)
    d = e / np.sum(e, axis=1, keepdims=True) - f64(tg)
    dt1 = d.T
    dj = dt1 * f64(fj)
    r = wru.T @ xtu
    dm = (r - f64(tr1)) * f64(fm)
    djq = mxq(dj, 0, "e5m2")
    dmq = mxq(dm, 0, "e4m3")
    y = wou.T @ djq + wbu.T @ dmq
    words, scales = planes(y)
    return y, words, scales

@@ -1,0 +1,285 @@
+from contextlib import ExitStack
+
+import concourse.mybir as mybir
+from concourse.masks import make_identity
+
+F32 = mybir.dt.float32
+BF16 = mybir.dt.bfloat16
+I32 = mybir.dt.int32
+U8 = mybir.dt.uint8
+E4M3 = mybir.dt.float8_e4m3fn_x4
+E5M2 = mybir.dt.float8_e5m2_x4
+E2M1 = mybir.dt.float4_e2m1fn_x4
+ALU = mybir.AluOpType
+ACT = mybir.ActivationFunctionType
+AX = mybir.AxisListType
+
+P = 128
+PACK = 4
+W = 512
+NT = W // P
+FLOPS = 4 * 2 * W * W * W
+
+
+def tile_mix_errors_of_two_heads_back_pl_kernel(
+    tc, xt_words, xt_scales, wc_words, wc_scales, tg, fj, wo_words, wo_scales,
+    wr_words, wr_scales, tr1, fm, wb_words, wb_scales, out_0, out_1, out_2,
+):
+    nc = tc.nc
+    tiles = range(NT)
+
+    def cols(b, width=P):
+        return slice(b * width, (b + 1) * width)
+
+    with ExitStack() as ctx:
+        sb = ctx.enter_context(tc.tile_pool(name="sb", bufs=1))
+        ps = ctx.enter_context(tc.psum_pool(name="ps", bufs=1))
+        ctx.enter_context(tc.manual_schedule())
+
+        def new(name, shape, dtype):
+            return sb.tile(shape, dtype, name=name, align_bytes=64)
+
+        xt_w = new("xt_w", [P, 2 * W], U8)
+        wc_w = new("wc_w", [P, W], I32)
+        wr_w = new("wr_w", [P, W], I32)
+        wb_w = new("wb_w", [P, 2 * W], U8)
+        wo_w = new("wo_w", [P, 2 * W], U8)
+        first_s = new("first_s", [P, 2 * W], U8)
+        wr_s = new("wr_s", [P, W], U8)
+        back_s = new("back_s", [P, 2 * W], U8)
+        xt_s, wc_s = first_s[:, cols(0, W)], first_s[:, cols(1, W)]
+        wr_wd = new("wr_wd", [P, W], I32)
+        wr_sd = new("wr_sd", [P, W], U8)
+        wb_wd = new("wb_wd", [P, 2 * W], U8)
+        wo_wd = new("wo_wd", [P, 2 * W], U8)
+        back_sd = new("back_sd", [P, 2 * W], U8)
+        tg_half = [new("tg%d" % h, [P, 2 * W], F32) for h in range(2)]
+        tr_half = [new("tr%d" % h, [P, PACK * 2 * P], F32) for h in range(2)]
+        fj_t = new("fj_t", [P, PACK], F32)
+        fm_t = new("fm_t", [P, PACK], F32)
+        ident = new("ident", [P, P], F32)
+        warm = new("warm", [P, 1], F32)
+        warm_out = new("warm_out", [P, 1], F32)
+
+        def load_words(queue, dst, words):
+            flat = words[0] if words.ndim == 3 else words[0].rearrange("p c r -> p (c r)")
+            queue.dma_start(out=dst[:].bitcast(I32) if words.ndim == 3 else dst[:], in_=flat.bitcast(I32))
+
+        def load_scales(queue, plane, scales, quadrants):
+            for q in quadrants:
+                queue.dma_start(
+                    out=plane[32 * q : 32 * q + 4, :].bitcast(I32), in_=scales[0, 4 * q : 4 * q + 4, :].bitcast(I32)
+                )
+
+        nc.vector.memset(first_s[:].bitcast(I32), 0)
+        nc.vector.memset(warm[:], 0.0)
+        nc.vector.memset(wr_s[:].bitcast(I32), 0)
+        nc.vector.memset(back_s[:].bitcast(I32), 0)
+        load_words(nc.sync, xt_w, xt_words)
+        load_words(nc.scalar, wc_w, wc_words)
+        load_scales(nc.sync, xt_s, xt_scales, range(4))
+        load_words(nc.scalar, wr_w, wr_words)
+        load_words(nc.scalar, wb_w, wb_words)
+        nc.scalar.activation(out=warm_out[:], in_=warm[:], func=ACT.Exp)
+        nc.gpsimd.dma_start(out=fm_t[:], in_=fm.rearrange("(p i) o -> p (i o)", i=PACK))
+        nc.gpsimd.dma_start(out=fj_t[:], in_=fj.rearrange("(p i) o -> p (i o)", i=PACK))
+        make_identity(nc, ident[:])
+        load_scales(nc.sync, wc_s, wc_scales, range(4))
+        tg_rows = tg.rearrange("(b p) j -> p b j", p=P)
+        tr_rows = tr1.rearrange("(p i) t -> p i t", i=PACK)
+
+        def load_tg(h):
+            nc.sync.dma_start(out=tg_half[h][:].rearrange("p (b j) -> p b j", b=2), in_=tg_rows[:, 2 * h : 2 * h + 2, :])
+
+        def load_tr(h):
+            nc.sync.dma_start(out=tr_half[h][:].rearrange("p (i t) -> p i t", i=PACK), in_=tr_rows[:, :, cols(h, 2 * P)])
+
+        load_tg(0)
+        load_scales(nc.sync, wr_s, wr_scales, range(4))
+        load_tr(0)
+        load_words(nc.sync, wo_w, wo_words)
+        load_tg(1)
+        load_tr(1)
+        load_scales(nc.sync, back_s[:, cols(0, W)], wb_scales, range(4))
+        load_scales(nc.sync, back_s[:, cols(1, W)], wo_scales, range(4))
+
+        def deal_fp4(dst, src):
+            nc.vector.tensor_copy(
+                out=dst[:].rearrange("p (i m h) -> p i m h", i=PACK, h=2),
+                in_=src[:].rearrange("p (m i h) -> p i m h", i=PACK, h=2),
+            )
+
+        nc.vector.tensor_copy(
+            out=wr_wd[:].rearrange("p (i m) -> p i m", i=PACK), in_=wr_w[:].rearrange("p (m i) -> p i m", i=PACK)
+        )
+        deal_fp4(wb_wd, wb_w)
+
+        score = [ps.tile([P, W], F32, name="score%d" % b, tag="mx%d" % b) for b in tiles]
+        for b in tiles:
+            nc.tensor.matmul_mx(
+                out=score[b][:],
+                lhsT=xt_w[:, cols(b, 2 * P)].bitcast(E2M1), lhsT_scale=xt_s[:, cols(b)],
+                rhs=wc_w[:].bitcast(E4M3), rhs_scale=wc_s,
+                start=True, stop=True,
+            )
+
+        neg_tg = [new("neg_tg%d" % b, [P, W], F32) for b in tiles]
+        tr_fm = [new("tr_fm%d" % h, [P, PACK * 2 * P], F32) for h in range(2)]
+        for h in range(2):
+            for b in (2 * h, 2 * h + 1):
+                nc.gpsimd.tensor_scalar(
+                    out=neg_tg[b][:].rearrange("t (i p) -> t i p", i=PACK),
+                    in0=tg_half[h][:, cols(b % 2, W)].rearrange("t (p i) -> t i p", i=PACK),
+                    scalar1=-1.0, scalar2=0.0, op0=ALU.mult, op1=ALU.add,
+                )
+            for i in range(PACK):
+                nc.gpsimd.tensor_scalar(
+                    out=tr_fm[h][:, cols(i, 2 * P)], in0=tr_half[h][:, cols(i, 2 * P)],
+                    scalar1=fm_t[:, i : i + 1], scalar2=0.0, op0=ALU.mult, op1=ALU.add,
+                )
+
+        neg_max = [new("neg_max%d" % b, [P, 1], F32) for b in tiles]
+        total = [new("total%d" % b, [P, 1], F32) for b in tiles]
+        inv_total = [new("inv_total%d" % b, [P, 1], F32) for b in tiles]
+        expo = [new("expo%d" % b, [P, W], F32) for b in tiles]
+        for b in tiles:
+            nc.vector.tensor_reduce(out=neg_max[b][:], in_=score[b][:], axis=AX.X, op=ALU.max, negate=True)
+            nc.scalar.activation(
+                out=expo[b][:].rearrange("t (i p) -> t i p", i=PACK),
+                in_=score[b][:].rearrange("t (p i) -> t i p", i=PACK),
+                func=ACT.Exp, bias=neg_max[b][:], scale=1.0, accum_out=total[b][:],
+            )
+            if b == 1:
+                nc.vector.tensor_copy(
+                    out=wr_sd[:].rearrange("p (i m) -> p i m", i=PACK),
+                    in_=wr_s[:].rearrange("p (m i) -> p i m", i=PACK),
+                )
+        for b in range(NT - 1):
+            nc.vector.reciprocal(out=inv_total[b][:], in_=total[b][:])
+        deal_fp4(wo_wd, wo_w)
+        nc.vector.reciprocal(out=inv_total[NT - 1][:], in_=total[NT - 1][:])
+
+        err_t = [ps.tile([P, W], F32, name="err_t%d" % b, tag="tr%d" % b) for b in tiles]
+
+        def add_transposed(b, src, first):
+            for i in range(PACK):
+                nc.tensor.matmul(
+                    out=err_t[b][:, cols(i)], lhsT=src[:, cols(i)], rhs=ident[:], is_transpose=True,
+                    start=(first and i == 0), stop=(not first and i == PACK - 1),
+                )
+
+        reg = [None] * NT
+
+        def regress(b):
+            reg[b] = ps.tile([P, W], F32, name="reg%d" % b, tag="mx%d" % b)
+            for i in range(PACK):
+                nc.tensor.matmul_mx(
+                    out=reg[b][:, cols(i)],
+                    lhsT=wr_wd[:, cols(i)].bitcast(E4M3), lhsT_scale=wr_sd[:, cols(i)],
+                    rhs=xt_w[:, cols(b, 2 * P)].bitcast(E2M1), rhs_scale=xt_s[:, cols(b)],
+                    start=True, stop=True,
+                )
+
+        add_transposed(0, neg_tg[0], True)
+        add_transposed(1, neg_tg[1], True)
+        for b in tiles:
+            regress(b)
+        add_transposed(2, neg_tg[2], True)
+        add_transposed(3, neg_tg[3], True)
+
+        share = [new("share%d" % b, [P, W], F32) for b in tiles]
+        for b in tiles:
+            nc.scalar.activation(out=share[b][:], in_=expo[b][:], func=ACT.Copy, scale=inv_total[b][:])
+            add_transposed(b, share[b], False)
+
+        dm_rows = [new("dm_rows%d" % b, [P, W], BF16) for b in tiles]
+        dm_in = [new("dm_in%d" % h, [P, 2 * W], BF16) for h in range(2)]
+        for b in tiles:
+            for i in range(PACK):
+                nc.vector.scalar_tensor_tensor(
+                    out=dm_rows[b][:, cols(i)], in0=reg[b][:, cols(i)], scalar=fm_t[:, i : i + 1],
+                    in1=tr_fm[b // 2][:, cols(2 * i + b % 2)], op0=ALU.mult, op1=ALU.subtract,
+                )
+            nc.scalar.copy(
+                out=dm_in[b // 2][:, cols(b % 2, W)].rearrange("p (t i) -> p t i", i=PACK),
+                in_=dm_rows[b][:].rearrange("p (i t) -> p t i", i=PACK),
+            )
+            if b == 1:
+                nc.vector.tensor_copy(
+                    out=back_sd[:].rearrange("p (w i m) -> p w i m", w=2, i=PACK),
+                    in_=back_s[:].rearrange("p (w m i) -> p w i m", w=2, i=PACK),
+                )
+
+        dm_w = new("dm_w", [P, W], I32)
+        dm_s = new("dm_s", [P, W], U8)
+        dj_w = new("dj_w", [P, W], I32)
+        dj_s = new("dj_s", [P, W], U8)
+        dj_in = [new("dj_in%d" % b, [P, W], BF16) for b in tiles]
+
+        def class_error(b):
+            nc.vector.tensor_tensor(
+                out=dj_in[b][:].rearrange("p (t i) -> p t i", i=PACK),
+                in0=err_t[b][:].rearrange("p (i t) -> p t i", i=PACK),
+                in1=fj_t[:].unsqueeze(1).to_broadcast([P, P, PACK]),
+                op=ALU.mult,
+            )
+
+        def quantize_dj(b):
+            nc.vector.quantize_mx(out=dj_w[:, cols(b)].bitcast(E5M2), scales=dj_s[:, cols(b)], in_=dj_in[b][:])
+
+        def quantize_dm(h):
+            nc.vector.quantize_mx(
+                out=dm_w[:, cols(h, 2 * P)].bitcast(E4M3), scales=dm_s[:, cols(h, 2 * P)], in_=dm_in[h][:]
+            )
+
+        class_error(0)
+        quantize_dm(0)
+        class_error(1)
+        quantize_dm(1)
+        class_error(2)
+        quantize_dj(0)
+        quantize_dj(1)
+        class_error(3)
+        quantize_dj(2)
+        quantize_dj(3)
+
+        acc = [ps.tile([P, W], F32, name="acc%d" % i, tag="mx%d" % i) for i in range(PACK)]
+        for i in range(PACK):
+            nc.tensor.matmul_mx(
+                out=acc[i][:],
+                lhsT=wb_wd[:, cols(i, 2 * P)].bitcast(E2M1), lhsT_scale=back_sd[:, cols(i)],
+                rhs=dm_w[:].bitcast(E4M3), rhs_scale=dm_s[:],
+                start=True, stop=False,
+            )
+        y = new("y", [P, PACK * W], F32)
+        out_rows = out_0.rearrange("(p i) t -> p i t", i=PACK)
+        for i in range(PACK):
+            nc.tensor.matmul_mx(
+                out=acc[i][:],
+                lhsT=wo_wd[:, cols(i, 2 * P)].bitcast(E2M1), lhsT_scale=back_sd[:, cols(PACK + i)],
+                rhs=dj_w[:].bitcast(E5M2), rhs_scale=dj_s[:],
+                start=False, stop=True,
+            )
+            if i % 2 == 0:
+                nc.scalar.copy(out=y[:, cols(i, W)], in_=acc[i][:])
+            else:
+                nc.vector.tensor_copy(out=y[:, cols(i, W)], in_=acc[i][:])
+            nc.sync.dma_start(out=out_rows[:, i, :], in_=y[:, cols(i, W)])
+
+        y_in = [new("y_in%d" % h, [P, 2 * W], BF16) for h in range(2)]
+        y_w = [new("y_w%d" % h, [P, 2 * P], I32) for h in range(2)]
+        y_s = new("y_s", [P, W], U8)
+        y_rows = y[:].rearrange("p (i t) -> p t i", i=PACK)
+        for b in tiles:
+            dst = y_in[b // 2][:, cols(b % 2, W)].rearrange("p (t i) -> p t i", i=PACK)
+            if b == NT - 1:
+                nc.scalar.copy(out=dst, in_=y_rows[:, cols(b), :])
+            else:
+                nc.vector.tensor_copy(out=dst, in_=y_rows[:, cols(b), :])
+        words_out = out_1[0].rearrange("p c r -> p (c r)").bitcast(I32)
+        for h in range(2):
+            nc.vector.quantize_mx(out=y_w[h][:].bitcast(E4M3), scales=y_s[:, cols(h, 2 * P)], in_=y_in[h][:])
+            nc.sync.dma_start(out=words_out[:, cols(h, 2 * P)], in_=y_w[h][:])
+        for q in range(4):
+            queue = nc.scalar if q < 2 else nc.sync
+            queue.dma_start(out=out_2[0, 4 * q : 4 * q + 4, :].bitcast(I32), in_=y_s[32 * q : 32 * q + 4, :].bitcast(I32))

@@ -45,14 +45,15 @@ def tile_mix_errors_of_two_heads_back_pl_kernel(
         wb_w = new("wb_w", [P, 2 * W], U8)
         wo_w = new("wo_w", [P, 2 * W], U8)
         first_s = new("first_s", [P, 2 * W], U8)
-        wr_s = new("wr_s", [P, W], U8)
-        back_s = new("back_s", [P, 2 * W], U8)
-        xt_s, wc_s = first_s[:, cols(0, W)], first_s[:, cols(1, W)]
+        xt_s, wc_s = (first_s[:, cols(k, W)] for k in range(2))
+        late_s = new("late_s", [P, 3 * W], U8)
+        wr_s, wb_s, wo_s = (late_s[:, cols(k, W)] for k in range(3))
         wr_wd = new("wr_wd", [P, W], I32)
         wr_sd = new("wr_sd", [P, W], U8)
         wb_wd = new("wb_wd", [P, 2 * W], U8)
         wo_wd = new("wo_wd", [P, 2 * W], U8)
-        back_sd = new("back_sd", [P, 2 * W], U8)
+        wb_sd = new("wb_sd", [P, W], U8)
+        wo_sd = new("wo_sd", [P, W], U8)
         tg_half = [new("tg%d" % h, [P, 2 * W], F32) for h in range(2)]
         tr_half = [new("tr%d" % h, [P, PACK * 2 * P], F32) for h in range(2)]
         fj_t = new("fj_t", [P, PACK], F32)
@@ -71,20 +72,6 @@ def tile_mix_errors_of_two_heads_back_pl_kernel(
                     out=plane[32 * q : 32 * q + 4, :].bitcast(I32), in_=scales[0, 4 * q : 4 * q + 4, :].bitcast(I32)
                 )
 
-        nc.vector.memset(first_s[:].bitcast(I32), 0)
-        nc.vector.memset(warm[:], 0.0)
-        nc.vector.memset(wr_s[:].bitcast(I32), 0)
-        nc.vector.memset(back_s[:].bitcast(I32), 0)
-        load_words(nc.sync, xt_w, xt_words)
-        load_words(nc.scalar, wc_w, wc_words)
-        load_scales(nc.sync, xt_s, xt_scales, range(4))
-        load_words(nc.scalar, wr_w, wr_words)
-        load_words(nc.scalar, wb_w, wb_words)
-        nc.scalar.activation(out=warm_out[:], in_=warm[:], func=ACT.Exp)
-        nc.gpsimd.dma_start(out=fm_t[:], in_=fm.rearrange("(p i) o -> p (i o)", i=PACK))
-        nc.gpsimd.dma_start(out=fj_t[:], in_=fj.rearrange("(p i) o -> p (i o)", i=PACK))
-        make_identity(nc, ident[:])
-        load_scales(nc.sync, wc_s, wc_scales, range(4))
         tg_rows = tg.rearrange("(b p) j -> p b j", p=P)
         tr_rows = tr1.rearrange("(p i) t -> p i t", i=PACK)
 
@@ -94,70 +81,111 @@ def tile_mix_errors_of_two_heads_back_pl_kernel(
         def load_tr(h):
             nc.sync.dma_start(out=tr_half[h][:].rearrange("p (i t) -> p i t", i=PACK), in_=tr_rows[:, :, cols(h, 2 * P)])
 
-        load_tg(0)
+        nc.gpsimd.memset(first_s[:].bitcast(I32), 0)
+        nc.vector.memset(warm[:], 0.0)
+        nc.vector.memset(late_s[:].bitcast(I32), 0)
+        load_words(nc.sync, xt_w, xt_words)
+        load_scales(nc.sync, xt_s, xt_scales, (0,))
+        load_words(nc.sync, wc_w, wc_words)
+        load_scales(nc.sync, xt_s, xt_scales, (1, 2, 3))
+        load_scales(nc.sync, wc_s, wc_scales, (0, 1))
+        nc.scalar.activation(out=warm_out[:], in_=warm[:], func=ACT.Exp)
+        nc.gpsimd.dma_start(out=fm_t[:], in_=fm.rearrange("(p i) o -> p (i o)", i=PACK))
+        nc.gpsimd.dma_start(out=fj_t[:], in_=fj.rearrange("(p i) o -> p (i o)", i=PACK))
+        make_identity(nc, ident[:])
+        load_scales(nc.sync, wc_s, wc_scales, (2, 3))
         load_scales(nc.sync, wr_s, wr_scales, range(4))
+        load_words(nc.sync, wr_w, wr_words)
         load_tr(0)
-        load_words(nc.sync, wo_w, wo_words)
-        load_tg(1)
+        load_tg(0)
         load_tr(1)
-        load_scales(nc.sync, back_s[:, cols(0, W)], wb_scales, range(4))
-        load_scales(nc.sync, back_s[:, cols(1, W)], wo_scales, range(4))
+        load_words(nc.sync, wb_w, wb_words)
+        load_tg(1)
+        load_words(nc.sync, wo_w, wo_words)
+        load_scales(nc.sync, wb_s, wb_scales, range(4))
+        load_scales(nc.sync, wo_s, wo_scales, range(4))
 
         def deal_fp4(dst, src):
-            nc.vector.tensor_copy(
-                out=dst[:].rearrange("p (i m h) -> p i m h", i=PACK, h=2),
-                in_=src[:].rearrange("p (m i h) -> p i m h", i=PACK, h=2),
+            for half in range(2):
+                nc.gpsimd.tensor_copy(
+                    out=dst[:].rearrange("p (i m h) -> p i m h", i=PACK, h=2)[:, cols(half, 2)],
+                    in_=src[:].rearrange("p (m i h) -> p i m h", i=PACK, h=2)[:, cols(half, 2)],
+                )
+
+        def deal_bytes(engine, dst, src):
+            engine.tensor_copy(
+                out=dst[:].rearrange("p (i m) -> p i m", i=PACK), in_=src[:].rearrange("p (m i) -> p i m", i=PACK)
             )
 
-        nc.vector.tensor_copy(
-            out=wr_wd[:].rearrange("p (i m) -> p i m", i=PACK), in_=wr_w[:].rearrange("p (m i) -> p i m", i=PACK)
-        )
-        deal_fp4(wb_wd, wb_w)
+        def dealt_views(dst, src):
+            return (
+                dst.rearrange("p (i c n) -> p c i n", i=PACK, n=4),
+                src.rearrange("p (c n i) -> p c i n", i=PACK, n=4),
+            )
 
         score = [ps.tile([P, W], F32, name="score%d" % b, tag="mx%d" % b) for b in tiles]
         for b in tiles:
             nc.tensor.matmul_mx(
                 out=score[b][:],
                 lhsT=xt_w[:, cols(b, 2 * P)].bitcast(E2M1), lhsT_scale=xt_s[:, cols(b)],
-                rhs=wc_w[:].bitcast(E4M3), rhs_scale=wc_s,
+                rhs=wc_w[:].bitcast(E4M3), rhs_scale=wc_s[:],
                 start=True, stop=True,
             )
 
-        neg_tg = [new("neg_tg%d" % b, [P, W], F32) for b in tiles]
         tr_fm = [new("tr_fm%d" % h, [P, PACK * 2 * P], F32) for h in range(2)]
-        for h in range(2):
-            for b in (2 * h, 2 * h + 1):
-                nc.gpsimd.tensor_scalar(
-                    out=neg_tg[b][:].rearrange("t (i p) -> t i p", i=PACK),
-                    in0=tg_half[h][:, cols(b % 2, W)].rearrange("t (p i) -> t i p", i=PACK),
-                    scalar1=-1.0, scalar2=0.0, op0=ALU.mult, op1=ALU.add,
-                )
+
+        def scale_targets(h):
             for i in range(PACK):
                 nc.gpsimd.tensor_scalar(
                     out=tr_fm[h][:, cols(i, 2 * P)], in0=tr_half[h][:, cols(i, 2 * P)],
                     scalar1=fm_t[:, i : i + 1], scalar2=0.0, op0=ALU.mult, op1=ALU.add,
                 )
 
+        scale_targets(0)
+        scale_targets(1)
+        deal_fp4(wb_wd, wb_w)
+        deal_bytes(nc.gpsimd, wb_sd, wb_s)
+        deal_fp4(wo_wd, wo_w)
+
+        neg_tg = [new("neg_tg%d" % b, [P, W], F32) for b in tiles]
+
+        def negate_targets(b):
+            dst, src = dealt_views(neg_tg[b][:], tg_half[b // 2][:, cols(b % 2, W)])
+            nc.scalar.activation(out=dst, in_=src, func=ACT.Copy, scale=-1.0)
+
         neg_max = [new("neg_max%d" % b, [P, 1], F32) for b in tiles]
-        total = [new("total%d" % b, [P, 1], F32) for b in tiles]
-        inv_total = [new("inv_total%d" % b, [P, 1], F32) for b in tiles]
+        total = [new("total%d" % h, [P, 2], F32) for h in range(2)]
+        inv_total = [new("inv_total%d" % h, [P, 2], F32) for h in range(2)]
         expo = [new("expo%d" % b, [P, W], F32) for b in tiles]
-        for b in tiles:
+
+        def exponentials(b):
             nc.vector.tensor_reduce(out=neg_max[b][:], in_=score[b][:], axis=AX.X, op=ALU.max, negate=True)
             nc.scalar.activation(
                 out=expo[b][:].rearrange("t (i p) -> t i p", i=PACK),
                 in_=score[b][:].rearrange("t (p i) -> t i p", i=PACK),
-                func=ACT.Exp, bias=neg_max[b][:], scale=1.0, accum_out=total[b][:],
+                func=ACT.Exp, bias=neg_max[b][:], scale=1.0, accum_out=total[b // 2][:, b % 2 : b % 2 + 1],
             )
-            if b == 1:
-                nc.vector.tensor_copy(
-                    out=wr_sd[:].rearrange("p (i m) -> p i m", i=PACK),
-                    in_=wr_s[:].rearrange("p (m i) -> p i m", i=PACK),
+
+        exponentials(0)
+        exponentials(1)
+        dst, src = dealt_views(wr_wd[:], wr_w[:])
+        nc.vector.tensor_copy(out=dst, in_=src)
+        deal_bytes(nc.vector, wr_sd, wr_s)
+        negate_targets(0)
+        exponentials(2)
+        negate_targets(1)
+        nc.vector.reciprocal(out=inv_total[0][:], in_=total[0][:])
+        exponentials(3)
+
+        reg = [ps.tile([P, W], F32, name="reg%d" % k, tag="mx%d" % k) for k in tiles]
+        for h in range(2):
+            for i in range(PACK):
+                nc.tensor.matmul_mx(
+                    out=reg[2 * h + i // 2][:, cols(i % 2, 2 * P)],
+                    lhsT=wr_wd[:, cols(i)].bitcast(E4M3), lhsT_scale=wr_sd[:, cols(i)],
+                    rhs=xt_w[:, cols(h, W)].bitcast(E2M1), rhs_scale=xt_s[:, cols(h, 2 * P)],
+                    start=True, stop=True,
                 )
-        for b in range(NT - 1):
-            nc.vector.reciprocal(out=inv_total[b][:], in_=total[b][:])
-        deal_fp4(wo_wd, wo_w)
-        nc.vector.reciprocal(out=inv_total[NT - 1][:], in_=total[NT - 1][:])
 
         err_t = [ps.tile([P, W], F32, name="err_t%d" % b, tag="tr%d" % b) for b in tiles]
 
@@ -168,53 +196,42 @@ def tile_mix_errors_of_two_heads_back_pl_kernel(
                     start=(first and i == 0), stop=(not first and i == PACK - 1),
                 )
 
-        reg = [None] * NT
-
-        def regress(b):
-            reg[b] = ps.tile([P, W], F32, name="reg%d" % b, tag="mx%d" % b)
-            for i in range(PACK):
-                nc.tensor.matmul_mx(
-                    out=reg[b][:, cols(i)],
-                    lhsT=wr_wd[:, cols(i)].bitcast(E4M3), lhsT_scale=wr_sd[:, cols(i)],
-                    rhs=xt_w[:, cols(b, 2 * P)].bitcast(E2M1), rhs_scale=xt_s[:, cols(b)],
-                    start=True, stop=True,
-                )
-
-        add_transposed(0, neg_tg[0], True)
-        add_transposed(1, neg_tg[1], True)
-        for b in tiles:
-            regress(b)
-        add_transposed(2, neg_tg[2], True)
-        add_transposed(3, neg_tg[3], True)
-
         share = [new("share%d" % b, [P, W], F32) for b in tiles]
-        for b in tiles:
-            nc.scalar.activation(out=share[b][:], in_=expo[b][:], func=ACT.Copy, scale=inv_total[b][:])
-            add_transposed(b, share[b], False)
 
-        dm_rows = [new("dm_rows%d" % b, [P, W], BF16) for b in tiles]
-        dm_in = [new("dm_in%d" % h, [P, 2 * W], BF16) for h in range(2)]
-        for b in tiles:
-            for i in range(PACK):
-                nc.vector.scalar_tensor_tensor(
-                    out=dm_rows[b][:, cols(i)], in0=reg[b][:, cols(i)], scalar=fm_t[:, i : i + 1],
-                    in1=tr_fm[b // 2][:, cols(2 * i + b % 2)], op0=ALU.mult, op1=ALU.subtract,
+        def shares(h):
+            for b in (2 * h, 2 * h + 1):
+                nc.vector.tensor_scalar(
+                    out=share[b][:], in0=expo[b][:], scalar1=inv_total[h][:, b % 2 : b % 2 + 1], scalar2=None,
+                    op0=ALU.mult,
                 )
-            nc.scalar.copy(
-                out=dm_in[b // 2][:, cols(b % 2, W)].rearrange("p (t i) -> p t i", i=PACK),
-                in_=dm_rows[b][:].rearrange("p (i t) -> p t i", i=PACK),
+
+        def transposes(b):
+            add_transposed(b, share[b], True)
+            add_transposed(b, neg_tg[b], False)
+
+        def interleave(copy, dst, src_rows):
+            copy(
+                out=dst.rearrange("p (c n i) -> p c i n", n=4, i=PACK),
+                in_=src_rows.rearrange("p i (c n) -> p c i n", n=4),
             )
-            if b == 1:
-                nc.vector.tensor_copy(
-                    out=back_sd[:].rearrange("p (w i m) -> p w i m", w=2, i=PACK),
-                    in_=back_s[:].rearrange("p (w m i) -> p w i m", w=2, i=PACK),
-                )
 
+        dm_rows = [new("dm_rows%d" % h, [P, 2 * W], BF16) for h in range(2)]
+        dm_in = [new("dm_in%d" % h, [P, 2 * W], BF16) for h in range(2)]
         dm_w = new("dm_w", [P, W], I32)
         dm_s = new("dm_s", [P, W], U8)
         dj_w = new("dj_w", [P, W], I32)
         dj_s = new("dj_s", [P, W], U8)
         dj_in = [new("dj_in%d" % b, [P, W], BF16) for b in tiles]
+
+        def regression_rows(h, rows):
+            for i in rows:
+                nc.vector.scalar_tensor_tensor(
+                    out=dm_rows[h][:, cols(i, 2 * P)], in0=reg[2 * h + i // 2][:, cols(i % 2, 2 * P)],
+                    scalar=fm_t[:, i : i + 1], in1=tr_fm[h][:, cols(i, 2 * P)], op0=ALU.mult, op1=ALU.subtract,
+                )
+
+        def interleave_dm(h):
+            interleave(nc.scalar.copy, dm_in[h][:], dm_rows[h][:].rearrange("p (i t) -> p i t", i=PACK))
 
         def class_error(b):
             nc.vector.tensor_tensor(
@@ -232,6 +249,20 @@ def tile_mix_errors_of_two_heads_back_pl_kernel(
                 out=dm_w[:, cols(h, 2 * P)].bitcast(E4M3), scales=dm_s[:, cols(h, 2 * P)], in_=dm_in[h][:]
             )
 
+        shares(0)
+        transposes(0)
+        transposes(1)
+        regression_rows(0, (0, 1))
+        nc.vector.reciprocal(out=inv_total[1][:], in_=total[1][:])
+        regression_rows(0, (2, 3))
+        interleave_dm(0)
+        shares(1)
+        negate_targets(2)
+        negate_targets(3)
+        transposes(2)
+        transposes(3)
+        regression_rows(1, range(PACK))
+        interleave_dm(1)
         class_error(0)
         quantize_dm(0)
         class_error(1)
@@ -239,6 +270,7 @@ def tile_mix_errors_of_two_heads_back_pl_kernel(
         class_error(2)
         quantize_dj(0)
         quantize_dj(1)
+        deal_bytes(nc.vector, wo_sd, wo_s)
         class_error(3)
         quantize_dj(2)
         quantize_dj(3)
@@ -247,7 +279,7 @@ def tile_mix_errors_of_two_heads_back_pl_kernel(
         for i in range(PACK):
             nc.tensor.matmul_mx(
                 out=acc[i][:],
-                lhsT=wb_wd[:, cols(i, 2 * P)].bitcast(E2M1), lhsT_scale=back_sd[:, cols(i)],
+                lhsT=wb_wd[:, cols(i, 2 * P)].bitcast(E2M1), lhsT_scale=wb_sd[:, cols(i)],
                 rhs=dm_w[:].bitcast(E4M3), rhs_scale=dm_s[:],
                 start=True, stop=False,
             )
@@ -256,7 +288,7 @@ def tile_mix_errors_of_two_heads_back_pl_kernel(
         for i in range(PACK):
             nc.tensor.matmul_mx(
                 out=acc[i][:],
-                lhsT=wo_wd[:, cols(i, 2 * P)].bitcast(E2M1), lhsT_scale=back_sd[:, cols(PACK + i)],
+                lhsT=wo_wd[:, cols(i, 2 * P)].bitcast(E2M1), lhsT_scale=wo_sd[:, cols(i)],
                 rhs=dj_w[:].bitcast(E5M2), rhs_scale=dj_s[:],
                 start=False, stop=True,
             )
@@ -269,13 +301,10 @@ def tile_mix_errors_of_two_heads_back_pl_kernel(
         y_in = [new("y_in%d" % h, [P, 2 * W], BF16) for h in range(2)]
         y_w = [new("y_w%d" % h, [P, 2 * P], I32) for h in range(2)]
         y_s = new("y_s", [P, W], U8)
-        y_rows = y[:].rearrange("p (i t) -> p t i", i=PACK)
+        y_rows = y[:].rearrange("p (i t) -> p i t", i=PACK)
         for b in tiles:
-            dst = y_in[b // 2][:, cols(b % 2, W)].rearrange("p (t i) -> p t i", i=PACK)
-            if b == NT - 1:
-                nc.scalar.copy(out=dst, in_=y_rows[:, cols(b), :])
-            else:
-                nc.vector.tensor_copy(out=dst, in_=y_rows[:, cols(b), :])
+            copy = nc.scalar.copy if b == NT - 1 else nc.vector.tensor_copy
+            interleave(copy, y_in[b // 2][:, cols(b % 2, W)], y_rows[:, :, cols(b)])
         words_out = out_1[0].rearrange("p c r -> p (c r)").bitcast(I32)
         for h in range(2):
             nc.vector.quantize_mx(out=y_w[h][:].bitcast(E4M3), scales=y_s[:, cols(h, 2 * P)], in_=y_in[h][:])

@@ -90,27 +90,26 @@ def tile_mix_errors_of_two_heads_back_pl_kernel(
         load_scales(nc.sync, xt_s, xt_scales, (1, 2, 3))
         load_scales(nc.sync, wc_s, wc_scales, (0, 1))
         nc.scalar.activation(out=warm_out[:], in_=warm[:], func=ACT.Exp)
+        load_words(nc.gpsimd, wb_w, wb_words)
+        load_words(nc.gpsimd, wo_w, wo_words)
         nc.gpsimd.dma_start(out=fm_t[:], in_=fm.rearrange("(p i) o -> p (i o)", i=PACK))
         nc.gpsimd.dma_start(out=fj_t[:], in_=fj.rearrange("(p i) o -> p (i o)", i=PACK))
         make_identity(nc, ident[:])
         load_scales(nc.sync, wc_s, wc_scales, (2, 3))
-        load_scales(nc.sync, wr_s, wr_scales, range(4))
         load_words(nc.sync, wr_w, wr_words)
+        load_scales(nc.sync, wr_s, wr_scales, range(4))
         load_tr(0)
         load_tg(0)
         load_tr(1)
-        load_words(nc.sync, wb_w, wb_words)
         load_tg(1)
-        load_words(nc.sync, wo_w, wo_words)
         load_scales(nc.sync, wb_s, wb_scales, range(4))
         load_scales(nc.sync, wo_s, wo_scales, range(4))
 
         def deal_fp4(dst, src):
-            for half in range(2):
-                nc.gpsimd.tensor_copy(
-                    out=dst[:].rearrange("p (i m h) -> p i m h", i=PACK, h=2)[:, cols(half, 2)],
-                    in_=src[:].rearrange("p (m i h) -> p i m h", i=PACK, h=2)[:, cols(half, 2)],
-                )
+            nc.vector.tensor_copy(
+                out=dst[:].rearrange("p (i m h) -> p i m h", i=PACK, h=2),
+                in_=src[:].rearrange("p (m i h) -> p i m h", i=PACK, h=2),
+            )
 
         def deal_bytes(engine, dst, src):
             engine.tensor_copy(
@@ -144,7 +143,6 @@ def tile_mix_errors_of_two_heads_back_pl_kernel(
         scale_targets(0)
         scale_targets(1)
         deal_fp4(wb_wd, wb_w)
-        deal_bytes(nc.gpsimd, wb_sd, wb_s)
         deal_fp4(wo_wd, wo_w)
 
         neg_tg = [new("neg_tg%d" % b, [P, W], F32) for b in tiles]
@@ -167,17 +165,13 @@ def tile_mix_errors_of_two_heads_back_pl_kernel(
             )
 
         exponentials(0)
-        exponentials(1)
         dst, src = dealt_views(wr_wd[:], wr_w[:])
         nc.vector.tensor_copy(out=dst, in_=src)
         deal_bytes(nc.vector, wr_sd, wr_s)
-        negate_targets(0)
-        exponentials(2)
-        negate_targets(1)
-        nc.vector.reciprocal(out=inv_total[0][:], in_=total[0][:])
-        exponentials(3)
+        for b in range(1, NT):
+            exponentials(b)
 
-        reg = [ps.tile([P, W], F32, name="reg%d" % k, tag="mx%d" % k) for k in tiles]
+        reg = [ps.tile([P, W], F32, name="reg%d" % k, tag="late%d" % k) for k in tiles]
         for h in range(2):
             for i in range(PACK):
                 nc.tensor.matmul_mx(
@@ -187,7 +181,7 @@ def tile_mix_errors_of_two_heads_back_pl_kernel(
                     start=True, stop=True,
                 )
 
-        err_t = [ps.tile([P, W], F32, name="err_t%d" % b, tag="tr%d" % b) for b in tiles]
+        err_t = [ps.tile([P, W], F32, name="err_t%d" % b, tag="mx%d" % b) for b in tiles]
 
         def add_transposed(b, src, first):
             for i in range(PACK):
@@ -206,8 +200,8 @@ def tile_mix_errors_of_two_heads_back_pl_kernel(
                 )
 
         def transposes(b):
-            add_transposed(b, share[b], True)
-            add_transposed(b, neg_tg[b], False)
+            add_transposed(b, neg_tg[b], True)
+            add_transposed(b, share[b], False)
 
         def interleave(copy, dst, src_rows):
             copy(
@@ -249,21 +243,20 @@ def tile_mix_errors_of_two_heads_back_pl_kernel(
                 out=dm_w[:, cols(h, 2 * P)].bitcast(E4M3), scales=dm_s[:, cols(h, 2 * P)], in_=dm_in[h][:]
             )
 
-        shares(0)
-        transposes(0)
-        transposes(1)
-        regression_rows(0, (0, 1))
-        nc.vector.reciprocal(out=inv_total[1][:], in_=total[1][:])
-        regression_rows(0, (2, 3))
-        interleave_dm(0)
-        shares(1)
-        negate_targets(2)
-        negate_targets(3)
-        transposes(2)
-        transposes(3)
-        regression_rows(1, range(PACK))
-        interleave_dm(1)
+        for b in range(NT - 1):
+            negate_targets(b)
+        for h in range(2):
+            nc.vector.reciprocal(out=inv_total[h][:], in_=total[h][:])
+            regression_rows(h, (0,))
+            shares(h)
+            regression_rows(h, range(1, PACK))
+            if h == 1:
+                negate_targets(NT - 1)
+            interleave_dm(h)
+            transposes(2 * h)
+            transposes(2 * h + 1)
         class_error(0)
+        deal_bytes(nc.vector, wb_sd, wb_s)
         quantize_dm(0)
         class_error(1)
         quantize_dm(1)
@@ -275,7 +268,7 @@ def tile_mix_errors_of_two_heads_back_pl_kernel(
         quantize_dj(2)
         quantize_dj(3)
 
-        acc = [ps.tile([P, W], F32, name="acc%d" % i, tag="mx%d" % i) for i in range(PACK)]
+        acc = [ps.tile([P, W], F32, name="acc%d" % i, tag="late%d" % i) for i in range(PACK)]
         for i in range(PACK):
             nc.tensor.matmul_mx(
                 out=acc[i][:],

@@ -17,8 +17,16 @@ AX = mybir.AxisListType
 P = 128
 PACK = 4
 W = 512
-NT = W // P
+HALF = W // 2
+TILES = W // P
+QUADRANTS = 4
+FP4_BYTES = 2
+RUN = 4
 FLOPS = 4 * 2 * W * W * W
+
+
+def part(index, width=P):
+    return slice(index * width, (index + 1) * width)
 
 
 def tile_mix_errors_of_two_heads_back_pl_kernel(
@@ -26,282 +34,293 @@ def tile_mix_errors_of_two_heads_back_pl_kernel(
     wr_words, wr_scales, tr1, fm, wb_words, wb_scales, out_0, out_1, out_2,
 ):
     nc = tc.nc
-    tiles = range(NT)
-
-    def cols(b, width=P):
-        return slice(b * width, (b + 1) * width)
 
     with ExitStack() as ctx:
-        sb = ctx.enter_context(tc.tile_pool(name="sb", bufs=1))
-        ps = ctx.enter_context(tc.psum_pool(name="ps", bufs=1))
+        sbuf = ctx.enter_context(tc.tile_pool(name="sbuf", bufs=1))
+        psum = ctx.enter_context(tc.psum_pool(name="psum", bufs=1))
         ctx.enter_context(tc.manual_schedule())
 
         def new(name, shape, dtype):
-            return sb.tile(shape, dtype, name=name, align_bytes=64)
+            return sbuf.tile(shape, dtype, name=name, align_bytes=64)
 
-        xt_w = new("xt_w", [P, 2 * W], U8)
+        def bank(name, tag):
+            return psum.tile([P, W], F32, name=name, tag=tag)
+
+        xt_w = new("xt_w", [P, FP4_BYTES * W], U8)
         wc_w = new("wc_w", [P, W], I32)
         wr_w = new("wr_w", [P, W], I32)
-        wb_w = new("wb_w", [P, 2 * W], U8)
-        wo_w = new("wo_w", [P, 2 * W], U8)
-        first_s = new("first_s", [P, 2 * W], U8)
-        xt_s, wc_s = (first_s[:, cols(k, W)] for k in range(2))
-        late_s = new("late_s", [P, 3 * W], U8)
-        wr_s, wb_s, wo_s = (late_s[:, cols(k, W)] for k in range(3))
-        wr_wd = new("wr_wd", [P, W], I32)
-        wr_sd = new("wr_sd", [P, W], U8)
-        wb_wd = new("wb_wd", [P, 2 * W], U8)
-        wo_wd = new("wo_wd", [P, 2 * W], U8)
-        wb_sd = new("wb_sd", [P, W], U8)
-        wo_sd = new("wo_sd", [P, W], U8)
-        tg_half = [new("tg%d" % h, [P, 2 * W], F32) for h in range(2)]
-        tr_half = [new("tr%d" % h, [P, PACK * 2 * P], F32) for h in range(2)]
-        fj_t = new("fj_t", [P, PACK], F32)
-        fm_t = new("fm_t", [P, PACK], F32)
-        ident = new("ident", [P, P], F32)
-        warm = new("warm", [P, 1], F32)
-        warm_out = new("warm_out", [P, 1], F32)
+        wb_w = new("wb_w", [P, FP4_BYTES * W], U8)
+        wo_w = new("wo_w", [P, FP4_BYTES * W], U8)
+        score_planes = new("score_planes", [P, 2 * W], U8)
+        xt_s, wc_s = (score_planes[:, part(c, W)] for c in range(2))
+        other_planes = new("other_planes", [P, 3 * W], U8)
+        wr_s, wb_s, wo_s = (other_planes[:, part(c, W)] for c in range(3))
+        wr_w_dealt = new("wr_w_dealt", [P, W], I32)
+        wr_s_dealt = new("wr_s_dealt", [P, W], U8)
+        wb_w_dealt = new("wb_w_dealt", [P, FP4_BYTES * W], U8)
+        wo_w_dealt = new("wo_w_dealt", [P, FP4_BYTES * W], U8)
+        wb_s_dealt = new("wb_s_dealt", [P, W], U8)
+        wo_s_dealt = new("wo_s_dealt", [P, W], U8)
+        tg_half = [new("tg_half%d" % h, [P, 2 * W], F32) for h in range(2)]
+        tr_half = [new("tr_half%d" % h, [P, PACK * HALF], F32) for h in range(2)]
+        fj_sb = new("fj_sb", [P, PACK], F32)
+        fm_sb = new("fm_sb", [P, PACK], F32)
+        identity = new("identity", [P, P], F32)
 
-        def load_words(queue, dst, words):
-            flat = words[0] if words.ndim == 3 else words[0].rearrange("p c r -> p (c r)")
-            queue.dma_start(out=dst[:].bitcast(I32) if words.ndim == 3 else dst[:], in_=flat.bitcast(I32))
+        def load_fp4(queue, dst, words):
+            queue.dma_start(out=dst[:].bitcast(I32), in_=words[0].bitcast(I32))
 
-        def load_scales(queue, plane, scales, quadrants):
+        def load_fp8(dst, words):
+            nc.sync.dma_start(out=dst[:], in_=words[0].rearrange("p c r -> p (c r)").bitcast(I32))
+
+        def load_scales(plane, scales, quadrants):
             for q in quadrants:
-                queue.dma_start(
-                    out=plane[32 * q : 32 * q + 4, :].bitcast(I32), in_=scales[0, 4 * q : 4 * q + 4, :].bitcast(I32)
-                )
+                nc.sync.dma_start(out=plane[32 * q : 32 * q + 4, :].bitcast(I32), in_=scales[0, part(q, 4), :].bitcast(I32))
 
-        tg_rows = tg.rearrange("(b p) j -> p b j", p=P)
-        tr_rows = tr1.rearrange("(p i) t -> p i t", i=PACK)
+        def load_factors(queue, dst, factors):
+            queue.dma_start(out=dst[:], in_=factors.rearrange("(p i) o -> p (i o)", i=PACK))
 
         def load_tg(h):
-            nc.sync.dma_start(out=tg_half[h][:].rearrange("p (b j) -> p b j", b=2), in_=tg_rows[:, 2 * h : 2 * h + 2, :])
+            nc.sync.dma_start(
+                out=tg_half[h][:].rearrange("t (b j) -> t b j", b=2),
+                in_=tg.rearrange("(b t) j -> t b j", t=P)[:, part(h, 2), :],
+            )
 
         def load_tr(h):
-            nc.sync.dma_start(out=tr_half[h][:].rearrange("p (i t) -> p i t", i=PACK), in_=tr_rows[:, :, cols(h, 2 * P)])
+            nc.sync.dma_start(
+                out=tr_half[h][:].rearrange("p (i t) -> p i t", i=PACK),
+                in_=tr1.rearrange("(p i) t -> p i t", i=PACK)[:, :, part(h, HALF)],
+            )
 
-        nc.gpsimd.memset(first_s[:].bitcast(I32), 0)
-        nc.vector.memset(warm[:], 0.0)
-        nc.vector.memset(late_s[:].bitcast(I32), 0)
-        load_words(nc.sync, xt_w, xt_words)
-        load_scales(nc.sync, xt_s, xt_scales, (0,))
-        load_words(nc.sync, wc_w, wc_words)
-        load_scales(nc.sync, xt_s, xt_scales, (1, 2, 3))
-        load_scales(nc.sync, wc_s, wc_scales, (0, 1))
-        nc.scalar.activation(out=warm_out[:], in_=warm[:], func=ACT.Exp)
-        load_words(nc.gpsimd, wb_w, wb_words)
-        load_words(nc.gpsimd, wo_w, wo_words)
-        nc.gpsimd.dma_start(out=fm_t[:], in_=fm.rearrange("(p i) o -> p (i o)", i=PACK))
-        nc.gpsimd.dma_start(out=fj_t[:], in_=fj.rearrange("(p i) o -> p (i o)", i=PACK))
-        make_identity(nc, ident[:])
-        load_scales(nc.sync, wc_s, wc_scales, (2, 3))
-        load_words(nc.sync, wr_w, wr_words)
-        load_scales(nc.sync, wr_s, wr_scales, range(4))
+        nc.gpsimd.memset(score_planes[:].bitcast(I32), 0)
+        nc.vector.memset(other_planes[:].bitcast(I32), 0)
+        load_fp4(nc.sync, xt_w, xt_words)
+        load_scales(xt_s, xt_scales, range(1))
+        load_fp8(wc_w, wc_words)
+        load_scales(xt_s, xt_scales, range(1, QUADRANTS))
+        load_scales(wc_s, wc_scales, range(QUADRANTS))
+        load_fp4(nc.gpsimd, wb_w, wb_words)
+        load_fp4(nc.gpsimd, wo_w, wo_words)
+        load_factors(nc.gpsimd, fj_sb, fj)
+        make_identity(nc, identity[:])
+        load_scales(wr_s, wr_scales, range(QUADRANTS))
+        load_fp8(wr_w, wr_words)
         load_tr(0)
+        load_factors(nc.sync, fm_sb, fm)
         load_tg(0)
         load_tr(1)
         load_tg(1)
-        load_scales(nc.sync, wb_s, wb_scales, range(4))
-        load_scales(nc.sync, wo_s, wo_scales, range(4))
+        load_scales(wb_s, wb_scales, range(QUADRANTS))
+        load_scales(wo_s, wo_scales, range(QUADRANTS))
 
-        def deal_fp4(dst, src):
+        def deal_fp4_words(dst, src):
             nc.vector.tensor_copy(
-                out=dst[:].rearrange("p (i m h) -> p i m h", i=PACK, h=2),
-                in_=src[:].rearrange("p (m i h) -> p i m h", i=PACK, h=2),
+                out=dst[:].rearrange("p (i c y) -> p i c y", i=PACK, y=FP4_BYTES),
+                in_=src[:].rearrange("p (c i y) -> p i c y", i=PACK, y=FP4_BYTES),
             )
 
-        def deal_bytes(engine, dst, src):
-            engine.tensor_copy(
-                out=dst[:].rearrange("p (i m) -> p i m", i=PACK), in_=src[:].rearrange("p (m i) -> p i m", i=PACK)
+        def deal_scale_bytes(dst, src):
+            nc.vector.tensor_copy(
+                out=dst[:].rearrange("p (i c) -> p i c", i=PACK), in_=src.rearrange("p (c i) -> p i c", i=PACK)
             )
 
-        def dealt_views(dst, src):
+        def dealing_views(dst, src):
             return (
-                dst.rearrange("p (i c n) -> p c i n", i=PACK, n=4),
-                src.rearrange("p (c n i) -> p c i n", i=PACK, n=4),
+                dst.rearrange("p (i g r) -> p g i r", i=PACK, r=RUN),
+                src.rearrange("p (g r i) -> p g i r", i=PACK, r=RUN),
             )
 
-        score = [ps.tile([P, W], F32, name="score%d" % b, tag="mx%d" % b) for b in tiles]
-        for b in tiles:
+        def interleave(copy, dst, rows):
+            copy(
+                out=dst.rearrange("p (g r i) -> p g i r", r=RUN, i=PACK),
+                in_=rows.rearrange("p i (g r) -> p g i r", r=RUN),
+            )
+
+        score = [bank("score%d" % b, "class%d" % b) for b in range(TILES)]
+        for b in range(TILES):
             nc.tensor.matmul_mx(
                 out=score[b][:],
-                lhsT=xt_w[:, cols(b, 2 * P)].bitcast(E2M1), lhsT_scale=xt_s[:, cols(b)],
-                rhs=wc_w[:].bitcast(E4M3), rhs_scale=wc_s[:],
+                lhsT=xt_w[:, part(b, FP4_BYTES * P)].bitcast(E2M1), lhsT_scale=xt_s[:, part(b)],
+                rhs=wc_w[:].bitcast(E4M3), rhs_scale=wc_s,
                 start=True, stop=True,
             )
 
-        tr_fm = [new("tr_fm%d" % h, [P, PACK * 2 * P], F32) for h in range(2)]
-
-        def scale_targets(h):
+        tr_fm = [new("tr_fm%d" % h, [P, PACK * HALF], F32) for h in range(2)]
+        for h in range(2):
             for i in range(PACK):
                 nc.gpsimd.tensor_scalar(
-                    out=tr_fm[h][:, cols(i, 2 * P)], in0=tr_half[h][:, cols(i, 2 * P)],
-                    scalar1=fm_t[:, i : i + 1], scalar2=0.0, op0=ALU.mult, op1=ALU.add,
+                    out=tr_fm[h][:, part(i, HALF)], in0=tr_half[h][:, part(i, HALF)],
+                    scalar1=fm_sb[:, i : i + 1], scalar2=0.0, op0=ALU.mult, op1=ALU.add,
                 )
 
-        scale_targets(0)
-        scale_targets(1)
-        deal_fp4(wb_wd, wb_w)
-        deal_fp4(wo_wd, wo_w)
+        deal_fp4_words(wb_w_dealt, wb_w)
+        deal_fp4_words(wo_w_dealt, wo_w)
+        deal_scale_bytes(wr_s_dealt, wr_s)
 
-        neg_tg = [new("neg_tg%d" % b, [P, W], F32) for b in tiles]
-
-        def negate_targets(b):
-            dst, src = dealt_views(neg_tg[b][:], tg_half[b // 2][:, cols(b % 2, W)])
-            nc.scalar.activation(out=dst, in_=src, func=ACT.Copy, scale=-1.0)
-
-        neg_max = [new("neg_max%d" % b, [P, 1], F32) for b in tiles]
+        neg_max = [new("neg_max%d" % b, [P, 1], F32) for b in range(TILES)]
         total = [new("total%d" % h, [P, 2], F32) for h in range(2)]
         inv_total = [new("inv_total%d" % h, [P, 2], F32) for h in range(2)]
-        expo = [new("expo%d" % b, [P, W], F32) for b in tiles]
+        expo = [new("expo%d" % b, [P, W], F32) for b in range(TILES)]
 
         def exponentials(b):
             nc.vector.tensor_reduce(out=neg_max[b][:], in_=score[b][:], axis=AX.X, op=ALU.max, negate=True)
             nc.scalar.activation(
                 out=expo[b][:].rearrange("t (i p) -> t i p", i=PACK),
                 in_=score[b][:].rearrange("t (p i) -> t i p", i=PACK),
-                func=ACT.Exp, bias=neg_max[b][:], scale=1.0, accum_out=total[b // 2][:, b % 2 : b % 2 + 1],
+                func=ACT.Exp, bias=neg_max[b][:], scale=1.0, accum_out=total[b // 2][:, part(b % 2, 1)],
             )
 
         exponentials(0)
-        dst, src = dealt_views(wr_wd[:], wr_w[:])
-        nc.vector.tensor_copy(out=dst, in_=src)
-        deal_bytes(nc.vector, wr_sd, wr_s)
-        for b in range(1, NT):
+        wr_out, wr_in = dealing_views(wr_w_dealt[:], wr_w[:])
+        nc.vector.tensor_copy(out=wr_out, in_=wr_in)
+        for b in range(1, TILES):
             exponentials(b)
 
-        reg = [ps.tile([P, W], F32, name="reg%d" % k, tag="late%d" % k) for k in tiles]
+        reg = [bank("reg%d" % c, "sum%d" % c) for c in range(PACK)]
+
+        def reg_part(h, i):
+            return reg[2 * h + i // 2][:, part(i % 2, HALF)]
+
         for h in range(2):
             for i in range(PACK):
                 nc.tensor.matmul_mx(
-                    out=reg[2 * h + i // 2][:, cols(i % 2, 2 * P)],
-                    lhsT=wr_wd[:, cols(i)].bitcast(E4M3), lhsT_scale=wr_sd[:, cols(i)],
-                    rhs=xt_w[:, cols(h, W)].bitcast(E2M1), rhs_scale=xt_s[:, cols(h, 2 * P)],
+                    out=reg_part(h, i),
+                    lhsT=wr_w_dealt[:, part(i)].bitcast(E4M3), lhsT_scale=wr_s_dealt[:, part(i)],
+                    rhs=xt_w[:, part(h, FP4_BYTES * HALF)].bitcast(E2M1), rhs_scale=xt_s[:, part(h, HALF)],
                     start=True, stop=True,
                 )
 
-        err_t = [ps.tile([P, W], F32, name="err_t%d" % b, tag="mx%d" % b) for b in tiles]
-
-        def add_transposed(b, src, first):
-            for i in range(PACK):
-                nc.tensor.matmul(
-                    out=err_t[b][:, cols(i)], lhsT=src[:, cols(i)], rhs=ident[:], is_transpose=True,
-                    start=(first and i == 0), stop=(not first and i == PACK - 1),
-                )
-
-        share = [new("share%d" % b, [P, W], F32) for b in tiles]
-
-        def shares(h):
-            for b in (2 * h, 2 * h + 1):
-                nc.vector.tensor_scalar(
-                    out=share[b][:], in0=expo[b][:], scalar1=inv_total[h][:, b % 2 : b % 2 + 1], scalar2=None,
-                    op0=ALU.mult,
-                )
-
-        def transposes(b):
-            add_transposed(b, neg_tg[b], True)
-            add_transposed(b, share[b], False)
-
-        def interleave(copy, dst, src_rows):
-            copy(
-                out=dst.rearrange("p (c n i) -> p c i n", n=4, i=PACK),
-                in_=src_rows.rearrange("p i (c n) -> p c i n", n=4),
-            )
-
-        dm_rows = [new("dm_rows%d" % h, [P, 2 * W], BF16) for h in range(2)]
-        dm_in = [new("dm_in%d" % h, [P, 2 * W], BF16) for h in range(2)]
+        d_t = [bank("d_t%d" % b, "class%d" % b) for b in range(TILES)]
+        neg_tg = [new("neg_tg%d" % b, [P, W], F32) for b in range(TILES)]
+        share = [new("share%d" % b, [P, W], F32) for b in range(TILES)]
+        dm_rows = [new("dm_rows%d" % h, [P, PACK * HALF], BF16) for h in range(2)]
+        dm_in = [new("dm_in%d" % h, [P, PACK * HALF], BF16) for h in range(2)]
         dm_w = new("dm_w", [P, W], I32)
         dm_s = new("dm_s", [P, W], U8)
         dj_w = new("dj_w", [P, W], I32)
         dj_s = new("dj_s", [P, W], U8)
-        dj_in = [new("dj_in%d" % b, [P, W], BF16) for b in tiles]
+        dj_in = [new("dj_in%d" % b, [P, PACK * P], BF16) for b in range(TILES)]
 
-        def regression_rows(h, rows):
-            for i in rows:
-                nc.vector.scalar_tensor_tensor(
-                    out=dm_rows[h][:, cols(i, 2 * P)], in0=reg[2 * h + i // 2][:, cols(i % 2, 2 * P)],
-                    scalar=fm_t[:, i : i + 1], in1=tr_fm[h][:, cols(i, 2 * P)], op0=ALU.mult, op1=ALU.subtract,
+        def negate_targets(b):
+            dealt, natural = dealing_views(neg_tg[b][:], tg_half[b // 2][:, part(b % 2, W)])
+            nc.scalar.activation(out=dealt, in_=natural, func=ACT.Copy, scale=-1.0)
+
+        def make_shares(h):
+            for c in range(2):
+                nc.vector.tensor_scalar(
+                    out=share[2 * h + c][:], in0=expo[2 * h + c][:], scalar1=inv_total[h][:, part(c, 1)], scalar2=None,
+                    op0=ALU.mult,
                 )
 
-        def interleave_dm(h):
-            interleave(nc.scalar.copy, dm_in[h][:], dm_rows[h][:].rearrange("p (i t) -> p i t", i=PACK))
+        def transpose_error(b):
+            terms = [(term, i) for term in (neg_tg[b], share[b]) for i in range(PACK)]
+            for step, (term, i) in enumerate(terms):
+                nc.tensor.matmul(
+                    out=d_t[b][:, part(i)], lhsT=term[:, part(i)], rhs=identity[:], is_transpose=True,
+                    start=(step == 0), stop=(step == len(terms) - 1),
+                )
 
-        def class_error(b):
+        def make_dm_rows(h, parts):
+            for i in parts:
+                nc.vector.scalar_tensor_tensor(
+                    out=dm_rows[h][:, part(i, HALF)], in0=reg_part(h, i), scalar=fm_sb[:, i : i + 1],
+                    in1=tr_fm[h][:, part(i, HALF)], op0=ALU.mult, op1=ALU.subtract,
+                )
+
+        for b in range(TILES - 1):
+            negate_targets(b)
+        for h in range(2):
+            nc.vector.reciprocal(out=inv_total[h][:], in_=total[h][:])
+            make_dm_rows(h, range(1))
+            make_shares(h)
+            make_dm_rows(h, range(1, PACK))
+            if h == 1:
+                negate_targets(TILES - 1)
+            interleave(nc.scalar.copy, dm_in[h][:], dm_rows[h][:].rearrange("p (i t) -> p i t", i=PACK))
+            transpose_error(2 * h)
+            transpose_error(2 * h + 1)
+
+        acc = [bank("acc%d" % i, "sum%d" % i) for i in range(PACK)]
+
+        def make_dj(b):
             nc.vector.tensor_tensor(
                 out=dj_in[b][:].rearrange("p (t i) -> p t i", i=PACK),
-                in0=err_t[b][:].rearrange("p (i t) -> p t i", i=PACK),
-                in1=fj_t[:].unsqueeze(1).to_broadcast([P, P, PACK]),
+                in0=d_t[b][:].rearrange("p (i t) -> p t i", i=PACK),
+                in1=fj_sb[:].unsqueeze(1).to_broadcast([P, P, PACK]),
                 op=ALU.mult,
             )
 
         def quantize_dj(b):
-            nc.vector.quantize_mx(out=dj_w[:, cols(b)].bitcast(E5M2), scales=dj_s[:, cols(b)], in_=dj_in[b][:])
+            nc.vector.quantize_mx(out=dj_w[:, part(b)].bitcast(E5M2), scales=dj_s[:, part(b)], in_=dj_in[b][:])
 
-        def quantize_dm(h):
+        def send_dm_back(h):
             nc.vector.quantize_mx(
-                out=dm_w[:, cols(h, 2 * P)].bitcast(E4M3), scales=dm_s[:, cols(h, 2 * P)], in_=dm_in[h][:]
+                out=dm_w[:, part(h, HALF)].bitcast(E4M3), scales=dm_s[:, part(h, HALF)], in_=dm_in[h][:]
             )
+            for i in range(PACK):
+                for b in (2 * h, 2 * h + 1):
+                    nc.tensor.matmul_mx(
+                        out=acc[i][:, part(b)],
+                        lhsT=wb_w_dealt[:, part(i, FP4_BYTES * P)].bitcast(E2M1), lhsT_scale=wb_s_dealt[:, part(i)],
+                        rhs=dm_w[:, part(b)].bitcast(E4M3), rhs_scale=dm_s[:, part(b)],
+                        start=(b == 0), stop=False,
+                    )
 
-        for b in range(NT - 1):
-            negate_targets(b)
-        for h in range(2):
-            nc.vector.reciprocal(out=inv_total[h][:], in_=total[h][:])
-            regression_rows(h, (0,))
-            shares(h)
-            regression_rows(h, range(1, PACK))
-            if h == 1:
-                negate_targets(NT - 1)
-            interleave_dm(h)
-            transposes(2 * h)
-            transposes(2 * h + 1)
-        class_error(0)
-        deal_bytes(nc.vector, wb_sd, wb_s)
-        quantize_dm(0)
-        class_error(1)
-        quantize_dm(1)
-        class_error(2)
+        make_dj(0)
+        deal_scale_bytes(wb_s_dealt, wb_s)
+        send_dm_back(0)
+        make_dj(1)
+        send_dm_back(1)
+        make_dj(2)
         quantize_dj(0)
         quantize_dj(1)
-        deal_bytes(nc.vector, wo_sd, wo_s)
-        class_error(3)
+        deal_scale_bytes(wo_s_dealt, wo_s)
+        make_dj(3)
         quantize_dj(2)
         quantize_dj(3)
 
-        acc = [ps.tile([P, W], F32, name="acc%d" % i, tag="late%d" % i) for i in range(PACK)]
-        for i in range(PACK):
-            nc.tensor.matmul_mx(
-                out=acc[i][:],
-                lhsT=wb_wd[:, cols(i, 2 * P)].bitcast(E2M1), lhsT_scale=wb_sd[:, cols(i)],
-                rhs=dm_w[:].bitcast(E4M3), rhs_scale=dm_s[:],
-                start=True, stop=False,
-            )
         y = new("y", [P, PACK * W], F32)
+        y_rows = y[:].rearrange("p (i t) -> p i t", i=PACK)
         out_rows = out_0.rearrange("(p i) t -> p i t", i=PACK)
-        for i in range(PACK):
+
+        def close_sum(i):
             nc.tensor.matmul_mx(
                 out=acc[i][:],
-                lhsT=wo_wd[:, cols(i, 2 * P)].bitcast(E2M1), lhsT_scale=wo_sd[:, cols(i)],
+                lhsT=wo_w_dealt[:, part(i, FP4_BYTES * P)].bitcast(E2M1), lhsT_scale=wo_s_dealt[:, part(i)],
                 rhs=dj_w[:].bitcast(E5M2), rhs_scale=dj_s[:],
                 start=False, stop=True,
             )
-            if i % 2 == 0:
-                nc.scalar.copy(out=y[:, cols(i, W)], in_=acc[i][:])
-            else:
-                nc.vector.tensor_copy(out=y[:, cols(i, W)], in_=acc[i][:])
-            nc.sync.dma_start(out=out_rows[:, i, :], in_=y[:, cols(i, W)])
 
-        y_in = [new("y_in%d" % h, [P, 2 * W], BF16) for h in range(2)]
-        y_w = [new("y_w%d" % h, [P, 2 * P], I32) for h in range(2)]
+        def empty(copy, i, tokens):
+            copy(out=y_rows[:, i, tokens], in_=acc[i][:, tokens])
+
+        def store(i, tokens):
+            nc.sync.dma_start(out=out_rows[:, i, tokens], in_=y_rows[:, i, tokens])
+
+        all_tokens = part(0, W)
+        close_sum(0)
+        for h in range(2):
+            empty(nc.scalar.copy, 0, part(h, HALF))
+            store(0, part(h, HALF))
+        for i, copy in ((1, nc.vector.tensor_copy), (2, nc.scalar.copy)):
+            close_sum(i)
+            empty(copy, i, all_tokens)
+            store(i, all_tokens)
+        close_sum(3)
+        empty(nc.vector.tensor_copy, 3, part(0, HALF))
+        empty(nc.scalar.copy, 3, part(1, HALF))
+        store(3, all_tokens)
+
+        y_in = [new("y_in%d" % h, [P, PACK * HALF], BF16) for h in range(2)]
+        y_w = [new("y_w%d" % h, [P, HALF], I32) for h in range(2)]
         y_s = new("y_s", [P, W], U8)
-        y_rows = y[:].rearrange("p (i t) -> p i t", i=PACK)
-        for b in tiles:
-            copy = nc.scalar.copy if b == NT - 1 else nc.vector.tensor_copy
-            interleave(copy, y_in[b // 2][:, cols(b % 2, W)], y_rows[:, :, cols(b)])
+        for b in range(TILES):
+            copy = nc.scalar.copy if b == TILES - 1 else nc.vector.tensor_copy
+            interleave(copy, y_in[b // 2][:, part(b % 2, PACK * P)], y_rows[:, :, part(b)])
         words_out = out_1[0].rearrange("p c r -> p (c r)").bitcast(I32)
         for h in range(2):
-            nc.vector.quantize_mx(out=y_w[h][:].bitcast(E4M3), scales=y_s[:, cols(h, 2 * P)], in_=y_in[h][:])
-            nc.sync.dma_start(out=words_out[:, cols(h, 2 * P)], in_=y_w[h][:])
-        for q in range(4):
-            queue = nc.scalar if q < 2 else nc.sync
-            queue.dma_start(out=out_2[0, 4 * q : 4 * q + 4, :].bitcast(I32), in_=y_s[32 * q : 32 * q + 4, :].bitcast(I32))
+            nc.vector.quantize_mx(out=y_w[h][:].bitcast(E4M3), scales=y_s[:, part(h, HALF)], in_=y_in[h][:])
+            nc.sync.dma_start(out=words_out[:, part(h, HALF)], in_=y_w[h][:])
+        for q in range(QUADRANTS):
+            queue = nc.scalar if q < QUADRANTS // 2 else nc.sync
+            queue.dma_start(out=out_2[0, part(q, 4), :].bitcast(I32), in_=y_s[32 * q : 32 * q + 4, :].bitcast(I32))

from contextlib import ExitStack

import concourse.mybir as mybir
from concourse.masks import make_identity

F32 = mybir.dt.float32
BF16 = mybir.dt.bfloat16
I32 = mybir.dt.int32
U8 = mybir.dt.uint8
E4M3 = mybir.dt.float8_e4m3fn_x4
E5M2 = mybir.dt.float8_e5m2_x4
E2M1 = mybir.dt.float4_e2m1fn_x4
ALU = mybir.AluOpType
ACT = mybir.ActivationFunctionType
AX = mybir.AxisListType

P = 128
PACK = 4
W = 512
HALF = W // 2
TILES = W // P
QUADRANTS = 4
FP4_BYTES = 2
RUN = 4
FLOPS = 4 * 2 * W * W * W


def part(index, width=P):
    return slice(index * width, (index + 1) * width)


def tile_mix_errors_of_two_heads_back_pl_kernel(
    tc, xt_words, xt_scales, wc_words, wc_scales, tg, fj, wo_words, wo_scales,
    wr_words, wr_scales, tr1, fm, wb_words, wb_scales, out_0, out_1, out_2,
):
    nc = tc.nc

    with ExitStack() as ctx:
        sbuf = ctx.enter_context(tc.tile_pool(name="sbuf", bufs=1))
        psum = ctx.enter_context(tc.psum_pool(name="psum", bufs=1))
        ctx.enter_context(tc.manual_schedule())

        def new(name, shape, dtype):
            return sbuf.tile(shape, dtype, name=name, align_bytes=64)

        def bank(name, tag):
            return psum.tile([P, W], F32, name=name, tag=tag)

        xt_w = new("xt_w", [P, FP4_BYTES * W], U8)
        wc_w = new("wc_w", [P, W], I32)
        wr_w = new("wr_w", [P, W], I32)
        wb_w = new("wb_w", [P, FP4_BYTES * W], U8)
        wo_w = new("wo_w", [P, FP4_BYTES * W], U8)
        score_planes = new("score_planes", [P, 2 * W], U8)
        xt_s, wc_s = (score_planes[:, part(c, W)] for c in range(2))
        other_planes = new("other_planes", [P, 3 * W], U8)
        wr_s, wb_s, wo_s = (other_planes[:, part(c, W)] for c in range(3))
        wr_w_dealt = new("wr_w_dealt", [P, W], I32)
        wr_s_dealt = new("wr_s_dealt", [P, W], U8)
        wb_w_dealt = new("wb_w_dealt", [P, FP4_BYTES * W], U8)
        wo_w_dealt = new("wo_w_dealt", [P, FP4_BYTES * W], U8)
        wb_s_dealt = new("wb_s_dealt", [P, W], U8)
        wo_s_dealt = new("wo_s_dealt", [P, W], U8)
        tg_half = [new("tg_half%d" % h, [P, 2 * W], F32) for h in range(2)]
        tr_half = [new("tr_half%d" % h, [P, PACK * HALF], F32) for h in range(2)]
        fj_sb = new("fj_sb", [P, PACK], F32)
        fm_sb = new("fm_sb", [P, PACK], F32)
        identity = new("identity", [P, P], F32)

        def load_fp4(queue, dst, words):
            queue.dma_start(out=dst[:].bitcast(I32), in_=words[0].bitcast(I32))

        def load_fp8(dst, words):
            nc.sync.dma_start(out=dst[:], in_=words[0].rearrange("p c r -> p (c r)").bitcast(I32))

        def load_scales(plane, scales, quadrants):
            for q in quadrants:
                nc.sync.dma_start(out=plane[32 * q : 32 * q + 4, :].bitcast(I32), in_=scales[0, part(q, 4), :].bitcast(I32))

        def load_factors(queue, dst, factors):
            queue.dma_start(out=dst[:], in_=factors.rearrange("(p i) o -> p (i o)", i=PACK))

        def load_tg(h):
            nc.sync.dma_start(
                out=tg_half[h][:].rearrange("t (b j) -> t b j", b=2),
                in_=tg.rearrange("(b t) j -> t b j", t=P)[:, part(h, 2), :],
            )

        def load_tr(h):
            nc.sync.dma_start(
                out=tr_half[h][:].rearrange("p (i t) -> p i t", i=PACK),
                in_=tr1.rearrange("(p i) t -> p i t", i=PACK)[:, :, part(h, HALF)],
            )

        nc.gpsimd.memset(score_planes[:].bitcast(I32), 0)
        nc.vector.memset(other_planes[:].bitcast(I32), 0)
        load_fp4(nc.sync, xt_w, xt_words)
        load_scales(xt_s, xt_scales, range(1))
        load_fp8(wc_w, wc_words)
        load_scales(xt_s, xt_scales, range(1, QUADRANTS))
        load_scales(wc_s, wc_scales, range(QUADRANTS))
        load_fp4(nc.gpsimd, wb_w, wb_words)
        load_fp4(nc.gpsimd, wo_w, wo_words)
        load_factors(nc.gpsimd, fj_sb, fj)
        make_identity(nc, identity[:])
        load_scales(wr_s, wr_scales, range(QUADRANTS))
        load_fp8(wr_w, wr_words)
        load_tr(0)
        load_factors(nc.sync, fm_sb, fm)
        load_tg(0)
        load_tr(1)
        load_tg(1)
        load_scales(wb_s, wb_scales, range(QUADRANTS))
        load_scales(wo_s, wo_scales, range(QUADRANTS))

        def deal_fp4_words(dst, src):
            nc.vector.tensor_copy(
                out=dst[:].rearrange("p (i c y) -> p i c y", i=PACK, y=FP4_BYTES),
                in_=src[:].rearrange("p (c i y) -> p i c y", i=PACK, y=FP4_BYTES),
            )

        def deal_scale_bytes(dst, src):
            nc.vector.tensor_copy(
                out=dst[:].rearrange("p (i c) -> p i c", i=PACK), in_=src.rearrange("p (c i) -> p i c", i=PACK)
            )

        def dealing_views(dst, src):
            return (
                dst.rearrange("p (i g r) -> p g i r", i=PACK, r=RUN),
                src.rearrange("p (g r i) -> p g i r", i=PACK, r=RUN),
            )

        def interleave(copy, dst, rows):
            copy(
                out=dst.rearrange("p (g r i) -> p g i r", r=RUN, i=PACK),
                in_=rows.rearrange("p i (g r) -> p g i r", r=RUN),
            )

        score = [bank("score%d" % b, "class%d" % b) for b in range(TILES)]
        for b in range(TILES):
            nc.tensor.matmul_mx(
                out=score[b][:],
                lhsT=xt_w[:, part(b, FP4_BYTES * P)].bitcast(E2M1), lhsT_scale=xt_s[:, part(b)],
                rhs=wc_w[:].bitcast(E4M3), rhs_scale=wc_s,
                start=True, stop=True,
            )

        tr_fm = [new("tr_fm%d" % h, [P, PACK * HALF], F32) for h in range(2)]
        for h in range(2):
            for i in range(PACK):
                nc.gpsimd.tensor_scalar(
                    out=tr_fm[h][:, part(i, HALF)], in0=tr_half[h][:, part(i, HALF)],
                    scalar1=fm_sb[:, i : i + 1], scalar2=0.0, op0=ALU.mult, op1=ALU.add,
                )

        deal_fp4_words(wb_w_dealt, wb_w)
        deal_fp4_words(wo_w_dealt, wo_w)
        deal_scale_bytes(wr_s_dealt, wr_s)

        neg_max = [new("neg_max%d" % b, [P, 1], F32) for b in range(TILES)]
        total = [new("total%d" % h, [P, 2], F32) for h in range(2)]
        inv_total = [new("inv_total%d" % h, [P, 2], F32) for h in range(2)]
        expo = [new("expo%d" % b, [P, W], F32) for b in range(TILES)]

        def exponentials(b):
            nc.vector.tensor_reduce(out=neg_max[b][:], in_=score[b][:], axis=AX.X, op=ALU.max, negate=True)
            nc.scalar.activation(
                out=expo[b][:].rearrange("t (i p) -> t i p", i=PACK),
                in_=score[b][:].rearrange("t (p i) -> t i p", i=PACK),
                func=ACT.Exp, bias=neg_max[b][:], scale=1.0, accum_out=total[b // 2][:, part(b % 2, 1)],
            )

        exponentials(0)
        wr_out, wr_in = dealing_views(wr_w_dealt[:], wr_w[:])
        nc.vector.tensor_copy(out=wr_out, in_=wr_in)
        for b in range(1, TILES):
            exponentials(b)

        reg = [bank("reg%d" % c, "sum%d" % c) for c in range(PACK)]

        def reg_part(h, i):
            return reg[2 * h + i // 2][:, part(i % 2, HALF)]

        for h in range(2):
            for i in range(PACK):
                nc.tensor.matmul_mx(
                    out=reg_part(h, i),
                    lhsT=wr_w_dealt[:, part(i)].bitcast(E4M3), lhsT_scale=wr_s_dealt[:, part(i)],
                    rhs=xt_w[:, part(h, FP4_BYTES * HALF)].bitcast(E2M1), rhs_scale=xt_s[:, part(h, HALF)],
                    start=True, stop=True,
                )

        d_t = [bank("d_t%d" % b, "class%d" % b) for b in range(TILES)]
        neg_tg = [new("neg_tg%d" % b, [P, W], F32) for b in range(TILES)]
        share = [new("share%d" % b, [P, W], F32) for b in range(TILES)]
        dm_rows = [new("dm_rows%d" % h, [P, PACK * HALF], BF16) for h in range(2)]
        dm_in = [new("dm_in%d" % h, [P, PACK * HALF], BF16) for h in range(2)]
        dm_w = new("dm_w", [P, W], I32)
        dm_s = new("dm_s", [P, W], U8)
        dj_w = new("dj_w", [P, W], I32)
        dj_s = new("dj_s", [P, W], U8)
        dj_in = [new("dj_in%d" % b, [P, PACK * P], BF16) for b in range(TILES)]

        def negate_targets(b):
            dealt, natural = dealing_views(neg_tg[b][:], tg_half[b // 2][:, part(b % 2, W)])
            nc.scalar.activation(out=dealt, in_=natural, func=ACT.Copy, scale=-1.0)

        def make_shares(h):
            for c in range(2):
                nc.vector.tensor_scalar(
                    out=share[2 * h + c][:], in0=expo[2 * h + c][:], scalar1=inv_total[h][:, part(c, 1)], scalar2=None,
                    op0=ALU.mult,
                )

        def transpose_error(b):
            terms = [(term, i) for term in (neg_tg[b], share[b]) for i in range(PACK)]
            for step, (term, i) in enumerate(terms):
                nc.tensor.matmul(
                    out=d_t[b][:, part(i)], lhsT=term[:, part(i)], rhs=identity[:], is_transpose=True,
                    start=(step == 0), stop=(step == len(terms) - 1),
                )

        def make_dm_rows(h, parts):
            for i in parts:
                nc.vector.scalar_tensor_tensor(
                    out=dm_rows[h][:, part(i, HALF)], in0=reg_part(h, i), scalar=fm_sb[:, i : i + 1],
                    in1=tr_fm[h][:, part(i, HALF)], op0=ALU.mult, op1=ALU.subtract,
                )

        for b in range(TILES - 1):
            negate_targets(b)
        for h in range(2):
            nc.vector.reciprocal(out=inv_total[h][:], in_=total[h][:])
            make_dm_rows(h, range(1))
            make_shares(h)
            make_dm_rows(h, range(1, PACK))
            if h == 1:
                negate_targets(TILES - 1)
            interleave(nc.scalar.copy, dm_in[h][:], dm_rows[h][:].rearrange("p (i t) -> p i t", i=PACK))
            transpose_error(2 * h)
            transpose_error(2 * h + 1)

        acc = [bank("acc%d" % i, "sum%d" % i) for i in range(PACK)]

        def make_dj(b):
            nc.vector.tensor_tensor(
                out=dj_in[b][:].rearrange("p (t i) -> p t i", i=PACK),
                in0=d_t[b][:].rearrange("p (i t) -> p t i", i=PACK),
                in1=fj_sb[:].unsqueeze(1).to_broadcast([P, P, PACK]),
                op=ALU.mult,
            )

        def quantize_dj(b):
            nc.vector.quantize_mx(out=dj_w[:, part(b)].bitcast(E5M2), scales=dj_s[:, part(b)], in_=dj_in[b][:])

        def send_dm_back(h):
            nc.vector.quantize_mx(
                out=dm_w[:, part(h, HALF)].bitcast(E4M3), scales=dm_s[:, part(h, HALF)], in_=dm_in[h][:]
            )
            for i in range(PACK):
                for b in (2 * h, 2 * h + 1):
                    nc.tensor.matmul_mx(
                        out=acc[i][:, part(b)],
                        lhsT=wb_w_dealt[:, part(i, FP4_BYTES * P)].bitcast(E2M1), lhsT_scale=wb_s_dealt[:, part(i)],
                        rhs=dm_w[:, part(b)].bitcast(E4M3), rhs_scale=dm_s[:, part(b)],
                        start=(b == 0), stop=False,
                    )

        make_dj(0)
        deal_scale_bytes(wb_s_dealt, wb_s)
        send_dm_back(0)
        make_dj(1)
        send_dm_back(1)
        make_dj(2)
        quantize_dj(0)
        quantize_dj(1)
        deal_scale_bytes(wo_s_dealt, wo_s)
        make_dj(3)
        quantize_dj(2)
        quantize_dj(3)

        y = new("y", [P, PACK * W], F32)
        y_rows = y[:].rearrange("p (i t) -> p i t", i=PACK)
        out_rows = out_0.rearrange("(p i) t -> p i t", i=PACK)

        def close_sum(i):
            nc.tensor.matmul_mx(
                out=acc[i][:],
                lhsT=wo_w_dealt[:, part(i, FP4_BYTES * P)].bitcast(E2M1), lhsT_scale=wo_s_dealt[:, part(i)],
                rhs=dj_w[:].bitcast(E5M2), rhs_scale=dj_s[:],
                start=False, stop=True,
            )

        def empty(copy, i, tokens):
            copy(out=y_rows[:, i, tokens], in_=acc[i][:, tokens])

        def store(i, tokens):
            nc.sync.dma_start(out=out_rows[:, i, tokens], in_=y_rows[:, i, tokens])

        all_tokens = part(0, W)
        close_sum(0)
        for h in range(2):
            empty(nc.scalar.copy, 0, part(h, HALF))
            store(0, part(h, HALF))
        for i, copy in ((1, nc.vector.tensor_copy), (2, nc.scalar.copy)):
            close_sum(i)
            empty(copy, i, all_tokens)
            store(i, all_tokens)
        close_sum(3)
        empty(nc.vector.tensor_copy, 3, part(0, HALF))
        empty(nc.scalar.copy, 3, part(1, HALF))
        store(3, all_tokens)

        y_in = [new("y_in%d" % h, [P, PACK * HALF], BF16) for h in range(2)]
        y_w = [new("y_w%d" % h, [P, HALF], I32) for h in range(2)]
        y_s = new("y_s", [P, W], U8)
        for b in range(TILES):
            copy = nc.scalar.copy if b == TILES - 1 else nc.vector.tensor_copy
            interleave(copy, y_in[b // 2][:, part(b % 2, PACK * P)], y_rows[:, :, part(b)])
        words_out = out_1[0].rearrange("p c r -> p (c r)").bitcast(I32)
        for h in range(2):
            nc.vector.quantize_mx(out=y_w[h][:].bitcast(E4M3), scales=y_s[:, part(h, HALF)], in_=y_in[h][:])
            nc.sync.dma_start(out=words_out[:, part(h, HALF)], in_=y_w[h][:])
        for q in range(QUADRANTS):
            queue = nc.scalar if q < QUADRANTS // 2 else nc.sync
            queue.dma_start(out=out_2[0, part(q, 4), :].bitcast(I32), in_=y_s[32 * q : 32 * q + 4, :].bitcast(I32))
